import numpy as np
import ml_dtypes


def mxq(x, axis, fmt="e4m3"):
    dtype, down = {"e4m3": (ml_dtypes.float8_e4m3fn, 7), "e5m2": (ml_dtypes.float8_e5m2, 14)}[fmt]
    v = np.moveaxis(np.asarray(x, np.float32).astype(ml_dtypes.bfloat16).astype(np.float64), axis, -1)
    blocks = v.reshape(v.shape[:-1] + (-1, 32))
    amax = np.abs(blocks).max(-1, keepdims=True)
    byte = np.maximum(np.where(amax > 0, np.frexp(amax)[1] - 1 + 127, 0) - down, 1)
    scale = np.exp2(byte - 127.0)
    codes = (blocks / scale).astype(np.float32).astype(dtype).astype(np.float64)
    return np.moveaxis((codes * scale).reshape(v.shape), -1, axis)


WIDE = False


def mx_kscale(k):
    if not WIDE:
        return np.ones(k)
    levels = np.array([10, -10, 5, -5, 0])
    if k % 512:
        return np.exp2(np.random.permutation(np.resize(levels, k // 32))).repeat(32)
    a = np.empty((k // 512, 16))
    for p in range(k // 512):
        a[p, :8] = np.random.permutation(np.resize(levels, 8))
        for g in range(8):
            far = levels[np.abs(levels - a[p, g]) >= 10]
            a[p, g + 8] = far[np.random.randint(len(far))]
    return np.exp2(a.ravel()).repeat(32)


def f64(x):
    return np.asarray(x).astype(np.float64)


def striped(idx):
    return np.tile(np.asarray(idx).reshape(-1, 16).T, (8, 1)).astype(np.uint16)


def unstriped(offs):
    return offs[:16].T.reshape(-1).astype(np.int64)


def striped8(idx):
    return np.asarray(idx).reshape(8, -1, 16).transpose(0, 2, 1).reshape(128, -1).astype(np.uint16)


def unstriped8(offs):
    return offs.reshape(8, 16, -1).transpose(0, 2, 1).reshape(8, -1).astype(np.int64)


def pick8(x, idx, run):
    r = np.arange(len(x))
    return x[r[:, None], idx[r % (8 * run) // run]]


E2M1 = np.array([0.0, 0.5, 1.0, 1.5, 2.0, 3.0, 4.0, 6.0, -0.0, -0.5, -1.0, -1.5, -2.0, -3.0, -4.0, -6.0])


def pack_weight(w, fmt):
    k, n = w.shape
    w = f64(np.asarray(w, np.float32).astype(ml_dtypes.bfloat16)).reshape(k // 32, 32, n)
    amax = np.abs(w).max(1)
    if fmt == "e4m3":
        byte = np.frexp(amax)[1] - 1 + 127 - 7
    else:
        mant, ex = np.frexp(amax / 6.0)
        byte = np.where(mant > 0.5, ex, ex - 1) + 127
    byte = np.clip(np.where(amax > 0, byte, 1), 1, 254)
    scaled = (w * np.exp2(127.0 - byte)[:, None, :]).reshape(k, n).astype(np.float32)
    by_word = np.ascontiguousarray(scaled.reshape(k // 512, 128, 4, n).transpose(0, 1, 3, 2))
    if fmt == "e4m3":
        words = by_word.astype(ml_dtypes.float8_e4m3fn).view(np.uint8)
    else:
        c = by_word.astype(ml_dtypes.float4_e2m1fn).view(np.uint8) & 0xF
        words = (c[..., 0::2] | (c[..., 1::2] << 4)).reshape(k // 512, 128, 2 * n)
    return np.ascontiguousarray(words), np.ascontiguousarray(byte.astype(np.uint8).reshape(k // 512, 16, n))


def unpack_weight(words, scales, fmt):
    g, _, n = scales.shape
    words = np.ascontiguousarray(words).reshape(g, 128, n, -1)
    if fmt == "e4m3":
        vals = words.view(ml_dtypes.float8_e4m3fn).astype(np.float64)
    else:
        nib = np.empty((g, 128, n, 4), np.uint8)
        nib[..., 0::2] = words & 0xF
        nib[..., 1::2] = words >> 4
        vals = E2M1[nib]
    vals = vals * np.repeat(np.exp2(scales.astype(np.float64) - 127.0), 8, axis=1)[..., None]
    return vals.transpose(0, 1, 3, 2).reshape(g * 512, n)


K, J, R, T, U, F, C, O, N = 512, 256, 512, 1024, 1024, 1024, 512, 128, 256


def setup_inputs():
    n = np.random.standard_normal
    idx = np.stack([np.random.permutation(T)[:J] for _ in range(8)])
    idx2 = np.stack([np.random.permutation(U)[:J] for _ in range(8)])
    idx3 = np.stack([np.random.permutation(U)[:J] for _ in range(8)])
    idx4 = np.random.permutation(F)[:R]
    idx5 = np.random.permutation(C)[:J]
    idx6 = np.random.permutation(C)[:O]
    idx7 = np.stack([np.random.permutation(C)[:O] for _ in range(8)])
    fk = mx_kscale(K)
    fr = mx_kscale(R)
    tr = np.ones(F)
    tr[idx4] = fr
    wtp = pack_weight(n((K, F)) * 1 / np.sqrt(K) / fk[:, None] * tr, "e4m3")
    wbp = pack_weight(n((R, N)) * 1 / np.sqrt(R) / fr[:, None], "e2m1")
    return {
        "ta": (np.random.randint(-7, 8, (K, T)).astype(np.float64)).astype(np.float32),
        "tb": (np.random.randint(-7, 8, (K, U)).astype(np.float64)).astype(np.float32),
        "ga": ((np.random.randint(8, 25, (K, 1)) / 64.0) * fk[:, None]).astype(np.float32),
        "gb": ((np.random.randint(8, 25, (K, 1)) / 64.0) * fk[:, None]).astype(np.float32),
        "gd": ((np.random.randint(8, 25, (K, 1)) / 64.0) * fk[:, None]).astype(np.float32),
        "wt_words": wtp[0],
        "wt_scales": wtp[1],
        "sa": (np.random.uniform(0.5, 1.6, (R, 1))).astype(np.float32),
        "sb": (np.random.uniform(0.5, 1.6, (R, 1))).astype(np.float32),
        "wb_words": wbp[0],
        "wb_scales": wbp[1],
        "offs": striped8(idx),
        "offs2": striped8(idx2),
        "offs3": striped8(idx3),
        "offs4": striped(idx4),
        "offs5": striped(idx5),
        "offs6": striped(idx6),
        "offs7": striped8(idx7),
    }


def reference(ta, tb, ga, gb, gd, wt_words, wt_scales, sa, sb, wb_words, wb_scales, offs, offs2, offs3, offs4, offs5, offs6, offs7):
    idx = unstriped8(offs)
    idx2 = unstriped8(offs2)
    idx3 = unstriped8(offs3)
    idx4 = unstriped(offs4)
    idx5 = unstriped(offs5)
    idx6 = unstriped(offs6)
    idx7 = unstriped8(offs7)
    wtu = unpack_weight(wt_words, wt_scales, "e4m3")
    wbu = unpack_weight(wb_words, wb_scales, "e2m1")
    xc = np.maximum(np.minimum(pick8(f64(ta), idx, 64) * f64(ga), pick8(f64(tb), idx2, 64) * f64(gb)), pick8(f64(tb), idx3, 64) * f64(gd))
    wtidx4g = wtu[:, idx4]
    xcq = mxq(xc, 0, "e4m3")
    a = wtidx4g.T @ xcq
    pw = np.zeros((R, C))
    pw[:, idx5] = a
    hid = np.maximum(pw[:, idx6] * f64(sa), pick8(pw, idx7, 64) * f64(sb))
    hidq = mxq(hid, 0, "e4m3")
    y = wbu.T @ hidq
    return y

@@ -1,0 +1,174 @@
+from contextlib import ExitStack
+
+import concourse.mybir as mybir
+
+F32 = mybir.dt.float32
+BF16 = mybir.dt.bfloat16
+I32 = mybir.dt.int32
+U32 = mybir.dt.uint32
+U16 = mybir.dt.uint16
+U8 = mybir.dt.uint8
+FP8X4 = mybir.dt.float8_e4m3fn_x4
+FP4X4 = mybir.dt.float4_e2m1fn_x4
+COPY = mybir.ActivationFunctionType.Copy
+MIN = mybir.AluOpType.min
+MAX = mybir.AluOpType.max
+
+K, J, R, T, U, F, C, O, N = 512, 256, 512, 1024, 1024, 1024, 512, 128, 256
+P = 128
+PACK = 4
+FLOPS = 2 * K * R * J + 2 * R * N * O
+
+
+def tile_picked_boundedcode_store_one_boardmixed_one_plain_kernel(
+    tc, ta, tb, ga, gb, gd, wt_words, wt_scales, sa, sb, wb_words, wb_scales,
+    offs, offs2, offs3, offs4, offs5, offs6, offs7, out,
+):
+    nc = tc.nc
+    with ExitStack() as ctx:
+        lists = ctx.enter_context(tc.tile_pool(name="lists", bufs=1))
+        pool = ctx.enter_context(tc.tile_pool(name="work", bufs=1))
+        psum = ctx.enter_context(tc.psum_pool(name="psum", bufs=1))
+
+        def list_tile(src, name):
+            tile = lists.tile([P, src.shape[1]], U16, name=name)
+            nc.sync.dma_start(tile[:], src)
+            return tile
+
+        def column_tile(src, name, queue):
+            tile = pool.tile([P, PACK], F32, name=name)
+            queue.dma_start(tile[:], src.rearrange("(p t) o -> p (t o)", t=PACK))
+            return tile
+
+        def table_tile(src, t, name):
+            tile = pool.tile([P, src.shape[1]], F32, name=name)
+            nc.sync.dma_start(tile[:], src.rearrange("(p t) c -> p t c", t=PACK)[:, t, :])
+            return tile
+
+        def scale_rows(src, name, queue):
+            width = src.shape[2]
+            rows = pool.tile([PACK, PACK, width // 4], I32, name=name)
+            queue.dma_start(rows[:], src[0].bitcast(I32).rearrange("(q i) c -> i q c", i=PACK))
+            return rows
+
+        def scale_plane(rows, name):
+            plane = pool.tile([P, rows.shape[2] * 4], U8, name=name, align_bytes=64)
+            nc.vector.memset(plane[:].bitcast(I32), 0)
+            for q in range(4):
+                nc.vector.tensor_copy(plane[32 * q : 32 * q + PACK, :].bitcast(I32), rows[:, q, :])
+            return plane
+
+        gb_t = column_tile(gb, "gb_t", nc.gpsimd)
+        gd_t = column_tile(gd, "gd_t", nc.gpsimd)
+        ga_t = column_tile(ga, "ga_t", nc.gpsimd)
+        wt_rows = scale_rows(wt_scales, "wt_rows", nc.gpsimd)
+        ta_t = [None] * PACK
+        tb_t = [None] * PACK
+        tb_t[0] = table_tile(tb, 0, "tb0")
+        l2 = list_tile(offs2, "l2")
+        l3 = list_tile(offs3, "l3")
+        ta_t[0] = table_tile(ta, 0, "ta0")
+        l1 = list_tile(offs, "l1")
+        tb_t[1] = table_tile(tb, 1, "tb1")
+        ta_t[1] = table_tile(ta, 1, "ta1")
+        wt_all = pool.tile([P, F], U32, name="wt_all")
+        nc.sync.dma_start(wt_all[:].bitcast(I32), wt_words[0].rearrange("p n t -> p (n t)").bitcast(I32))
+        l4 = list_tile(offs4, "l4")
+        for t in (2, 3):
+            tb_t[t] = table_tile(tb, t, "tb%d" % t)
+            ta_t[t] = table_tile(ta, t, "ta%d" % t)
+        l5 = list_tile(offs5, "l5")
+        l6 = list_tile(offs6, "l6")
+        l7 = list_tile(offs7, "l7")
+        sa_t = column_tile(sa, "sa_t", nc.sync)
+        sb_t = column_tile(sb, "sb_t", nc.sync)
+        wb_codes = pool.tile([P, 2 * N], U8, name="wb_codes", align_bytes=64)
+        nc.sync.dma_start(wb_codes[:].bitcast(I32), wb_words[0].bitcast(I32))
+        wb_rows = scale_rows(wb_scales, "wb_rows", nc.gpsimd)
+
+        board = [pool.tile([P, C], F32, name="board%d" % t) for t in range(PACK)]
+        for t in range(PACK):
+            nc.vector.memset(board[t][:], 0.0)
+        wt_plane = scale_plane(wt_rows, "wt_plane")
+        wb_plane = scale_plane(wb_rows, "wb_plane")
+
+        x_planes = pool.tile([P, PACK - 1, J], BF16, name="x_planes")
+        x_grouped = pool.tile([P, J, PACK], BF16, name="x_grouped", align_bytes=64)
+        x_codes = pool.tile([P, J], U32, name="x_codes", align_bytes=64)
+        x_scales = pool.tile([P, J], U8, name="x_scales", align_bytes=64)
+        w_codes = pool.tile([P, R], U32, name="w_codes", align_bytes=64)
+        w_scales = pool.tile([P, R], U8, name="w_scales", align_bytes=64)
+        halves = [slice(0, J // 2), slice(J // 2, J)]
+
+        for t in range(PACK):
+            upper = pool.tile([P, J], F32, name="upper%d" % t)
+            lower = pool.tile([P, J], F32, name="lower%d" % t)
+            coded = pool.tile([P, J], F32, name="coded%d" % t)
+            capped = pool.tile([P, J], F32, name="capped%d" % t)
+            nc.scalar.activation(upper[:], tb_t[t][:].indirect(l2[:]), COPY, scale=gb_t[:, t : t + 1])
+            nc.scalar.activation(lower[:], tb_t[t][:].indirect(l3[:]), COPY, scale=gd_t[:, t : t + 1])
+            nc.scalar.activation(coded[:], ta_t[t][:].indirect(l1[:]), COPY, scale=ga_t[:, t : t + 1])
+            if t < PACK - 1:
+                nc.vector.tensor_tensor(capped[:], coded[:], upper[:], MIN)
+                nc.vector.tensor_tensor(x_planes[:, t, :], capped[:], lower[:], MAX)
+            else:
+                for h in halves:
+                    nc.vector.tensor_tensor(capped[:, h], coded[:, h], upper[:, h], MIN)
+                for h in halves:
+                    nc.vector.tensor_tensor(x_grouped[:, h, t], capped[:, h], lower[:, h], MAX)
+            if t == 1:
+                nc.vector.tensor_copy(w_codes[:].rearrange("p (t m) -> p m t", t=PACK), wt_all[:].indirect(l4[:]))
+                nc.vector.tensor_copy(w_scales[:].rearrange("p (t m) -> p m t", t=PACK), wt_plane[:].indirect(l4[:]))
+            if t == PACK - 2:
+                nc.vector.tensor_copy(x_grouped[:, :, 0 : PACK - 1], x_planes[:].rearrange("p t j -> p j t"))
+        for h in halves:
+            nc.vector.quantize_mx(
+                x_codes[:, h].bitcast(FP8X4), x_scales[:, h], x_grouped[:, h, :].rearrange("p j t -> p (j t)")
+            )
+
+        hidden = [None] * PACK
+        for t in (0, 2, 3, 1):
+            bank = psum.tile([P, J], F32, name="bank%d" % t)
+            cols = slice(P * t, P * (t + 1))
+            nc.tensor.matmul_mx(
+                bank[:], lhsT=w_codes[:, cols].bitcast(FP8X4), lhsT_scale=w_scales[:, cols],
+                rhs=x_codes[:].bitcast(FP8X4), rhs_scale=x_scales[:], start=True, stop=True,
+            )
+            a_t = pool.tile([P, J], F32, name="a%d" % t)
+            if t == 0:
+                nc.vector.tensor_copy(a_t[:], bank[:])
+            else:
+                nc.scalar.copy(a_t[:], bank[:])
+            hidden[t] = a_t
+        for t in (0, 2, 3):
+            nc.vector.tensor_copy(board[t][:].indirect(l5[:]), hidden[t][:])
+        nc.scalar.activation(board[1][:].indirect(l5[:]), hidden[1][:], COPY)
+
+        first = pool.tile([P, PACK, O], F32, name="first")
+        second = pool.tile([P, PACK, O], F32, name="second")
+        h_planes = pool.tile([P, PACK - 1, O], BF16, name="h_planes")
+        h_grouped = pool.tile([P, O, PACK], BF16, name="h_grouped", align_bytes=64)
+        h_codes = pool.tile([P, O], U32, name="h_codes", align_bytes=64)
+        h_scales = pool.tile([P, O], U8, name="h_scales", align_bytes=64)
+        for t in range(PACK):
+            nc.scalar.activation(first[:, t, :], board[t][:].indirect(l6[:]), COPY, scale=sa_t[:, t : t + 1])
+            nc.scalar.activation(second[:, t, :], board[t][:].indirect(l7[:]), COPY, scale=sb_t[:, t : t + 1])
+        nc.vector.tensor_tensor(h_planes[:], first[:, 0:3, :], second[:, 0:3, :], MAX)
+        nc.vector.tensor_copy(h_grouped[:, :, 0:3], h_planes[:].rearrange("p t o -> p o t"))
+        nc.vector.tensor_tensor(h_grouped[:, :, 3], first[:, 3, :], second[:, 3, :], MAX)
+        nc.vector.quantize_mx(h_codes[:].bitcast(FP8X4), h_scales[:], h_grouped[:].rearrange("p o t -> p (o t)"))
+
+        for b in range(N // P):
+            bank = psum.tile([P, O], F32, name="ybank%d" % b)
+            nc.tensor.matmul_mx(
+                bank[:], lhsT=wb_codes[:, 2 * P * b : 2 * P * (b + 1)].bitcast(FP4X4),
+                lhsT_scale=wb_plane[:, P * b : P * (b + 1)],
+                rhs=h_codes[:].bitcast(FP8X4), rhs_scale=h_scales[:], start=True, stop=True,
+            )
+            y = pool.tile([P, O], F32, name="y%d" % b)
+            if b == 0:
+                nc.scalar.copy(y[:], bank[:])
+                nc.scalar.dma_start(out[P * b : P * (b + 1), :], y[:])
+            else:
+                nc.vector.tensor_copy(y[:], bank[:])
+                nc.sync.dma_start(out[P * b : P * (b + 1), :], y[:])

@@ -45,37 +45,28 @@ def tile_picked_boundedcode_store_one_boardmixed_one_plain_kernel(
             nc.sync.dma_start(tile[:], src.rearrange("(p t) c -> p t c", t=PACK)[:, t, :])
             return tile
 
-        def scale_rows(src, name, queue):
-            width = src.shape[2]
-            rows = pool.tile([PACK, PACK, width // 4], I32, name=name)
-            queue.dma_start(rows[:], src[0].bitcast(I32).rearrange("(q i) c -> i q c", i=PACK))
-            return rows
-
-        def scale_plane(rows, name):
-            plane = pool.tile([P, rows.shape[2] * 4], U8, name=name, align_bytes=64)
-            nc.vector.memset(plane[:].bitcast(I32), 0)
-            for q in range(4):
-                nc.vector.tensor_copy(plane[32 * q : 32 * q + PACK, :].bitcast(I32), rows[:, q, :])
-            return plane
-
-        gb_t = column_tile(gb, "gb_t", nc.gpsimd)
-        gd_t = column_tile(gd, "gd_t", nc.gpsimd)
-        ga_t = column_tile(ga, "ga_t", nc.gpsimd)
-        wt_rows = scale_rows(wt_scales, "wt_rows", nc.gpsimd)
         ta_t = [None] * PACK
         tb_t = [None] * PACK
+        gb_t = column_tile(gb, "gb_t", nc.scalar)
+        gd_t = column_tile(gd, "gd_t", nc.scalar)
         tb_t[0] = table_tile(tb, 0, "tb0")
         l2 = list_tile(offs2, "l2")
         l3 = list_tile(offs3, "l3")
-        ta_t[0] = table_tile(ta, 0, "ta0")
-        l1 = list_tile(offs, "l1")
         tb_t[1] = table_tile(tb, 1, "tb1")
-        ta_t[1] = table_tile(ta, 1, "ta1")
         wt_all = pool.tile([P, F], U32, name="wt_all")
         nc.sync.dma_start(wt_all[:].bitcast(I32), wt_words[0].rearrange("p n t -> p (n t)").bitcast(I32))
+        tb_t[2] = table_tile(tb, 2, "tb2")
+        wt_rows = pool.tile([P, 2, F // 4], I32, name="wt_rows")
+        for u in range(2):
+            nc.sync.dma_start(
+                wt_rows[64 * u : 64 * u + PACK, :, :],
+                wt_scales[0].bitcast(I32)[8 * u : 8 * (u + 1), :].rearrange("(q i) c -> i q c", i=PACK),
+            )
         l4 = list_tile(offs4, "l4")
-        for t in (2, 3):
-            tb_t[t] = table_tile(tb, t, "tb%d" % t)
+        tb_t[3] = table_tile(tb, 3, "tb3")
+        ga_t = column_tile(ga, "ga_t", nc.sync)
+        l1 = list_tile(offs, "l1")
+        for t in range(PACK):
             ta_t[t] = table_tile(ta, t, "ta%d" % t)
         l5 = list_tile(offs5, "l5")
         l6 = list_tile(offs6, "l6")
@@ -84,15 +75,23 @@ def tile_picked_boundedcode_store_one_boardmixed_one_plain_kernel(
         sb_t = column_tile(sb, "sb_t", nc.sync)
         wb_codes = pool.tile([P, 2 * N], U8, name="wb_codes", align_bytes=64)
         nc.sync.dma_start(wb_codes[:].bitcast(I32), wb_words[0].bitcast(I32))
-        wb_rows = scale_rows(wb_scales, "wb_rows", nc.gpsimd)
+        wb_plane = pool.tile([P, N], U8, name="wb_plane", align_bytes=64)
+        nc.vector.memset(wb_plane[:].bitcast(I32), 0)
+        for q in range(4):
+            nc.sync.dma_start(
+                wb_plane[32 * q : 32 * q + PACK, :].bitcast(I32), wb_scales[0].bitcast(I32)[PACK * q : PACK * (q + 1), :]
+            )
 
         board = [pool.tile([P, C], F32, name="board%d" % t) for t in range(PACK)]
         for t in range(PACK):
             nc.vector.memset(board[t][:], 0.0)
-        wt_plane = scale_plane(wt_rows, "wt_plane")
-        wb_plane = scale_plane(wb_rows, "wb_plane")
+        wt_plane = pool.tile([P, F], U8, name="wt_plane")
+        nc.vector.memset(wt_plane[:].bitcast(I32), 0)
+        for q in range(4):
+            nc.vector.tensor_copy(
+                wt_plane[32 * q : 32 * q + PACK, :].bitcast(I32), wt_rows[64 * (q // 2) : 64 * (q // 2) + PACK, q % 2, :]
+            )
 
-        x_planes = pool.tile([P, PACK - 1, J], BF16, name="x_planes")
         x_grouped = pool.tile([P, J, PACK], BF16, name="x_grouped", align_bytes=64)
         x_codes = pool.tile([P, J], U32, name="x_codes", align_bytes=64)
         x_scales = pool.tile([P, J], U8, name="x_scales", align_bytes=64)
@@ -100,66 +99,97 @@ def tile_picked_boundedcode_store_one_boardmixed_one_plain_kernel(
         w_scales = pool.tile([P, R], U8, name="w_scales", align_bytes=64)
         halves = [slice(0, J // 2), slice(J // 2, J)]
 
+        nc.vector.tensor_copy(w_codes[:].rearrange("p (t m) -> p m t", t=PACK), wt_all[:].indirect(l4[:]))
+        nc.vector.tensor_copy(w_scales[:].rearrange("p (t m) -> p m t", t=PACK), wt_plane[:].indirect(l4[:]))
+
+        upper = pool.tile([P, PACK, J], F32, name="upper")
+        lower = pool.tile([P, PACK, J], F32, name="lower")
+        coded = pool.tile([P, PACK, J], F32, name="coded")
+        capped = pool.tile([P, PACK, J], F32, name="capped")
+
+        def bounds(t):
+            nc.scalar.activation(upper[:, t, :], tb_t[t][:].indirect(l2[:]), COPY, scale=gb_t[:, t : t + 1])
+            nc.scalar.activation(lower[:, t, :], tb_t[t][:].indirect(l3[:]), COPY, scale=gd_t[:, t : t + 1])
+
+        def codes(t):
+            nc.scalar.activation(coded[:, t, :], ta_t[t][:].indirect(l1[:]), COPY, scale=ga_t[:, t : t + 1])
+
+        def cap(t, cols):
+            nc.vector.tensor_tensor(capped[:, t, cols], coded[:, t, cols], upper[:, t, cols], MIN)
+
+        def floor_pair(t, cols):
+            nc.vector.tensor_tensor(
+                x_grouped[:, cols, t : t + 2],
+                capped[:, t : t + 2, cols].rearrange("p t j -> p j t"),
+                lower[:, t : t + 2, cols].rearrange("p t j -> p j t"),
+                MAX,
+            )
+
+        everything = slice(0, J)
         for t in range(PACK):
-            upper = pool.tile([P, J], F32, name="upper%d" % t)
-            lower = pool.tile([P, J], F32, name="lower%d" % t)
-            coded = pool.tile([P, J], F32, name="coded%d" % t)
-            capped = pool.tile([P, J], F32, name="capped%d" % t)
-            nc.scalar.activation(upper[:], tb_t[t][:].indirect(l2[:]), COPY, scale=gb_t[:, t : t + 1])
-            nc.scalar.activation(lower[:], tb_t[t][:].indirect(l3[:]), COPY, scale=gd_t[:, t : t + 1])
-            nc.scalar.activation(coded[:], ta_t[t][:].indirect(l1[:]), COPY, scale=ga_t[:, t : t + 1])
-            if t < PACK - 1:
-                nc.vector.tensor_tensor(capped[:], coded[:], upper[:], MIN)
-                nc.vector.tensor_tensor(x_planes[:, t, :], capped[:], lower[:], MAX)
-            else:
-                for h in halves:
-                    nc.vector.tensor_tensor(capped[:, h], coded[:, h], upper[:, h], MIN)
-                for h in halves:
-                    nc.vector.tensor_tensor(x_grouped[:, h, t], capped[:, h], lower[:, h], MAX)
-            if t == 1:
-                nc.vector.tensor_copy(w_codes[:].rearrange("p (t m) -> p m t", t=PACK), wt_all[:].indirect(l4[:]))
-                nc.vector.tensor_copy(w_scales[:].rearrange("p (t m) -> p m t", t=PACK), wt_plane[:].indirect(l4[:]))
-            if t == PACK - 2:
-                nc.vector.tensor_copy(x_grouped[:, :, 0 : PACK - 1], x_planes[:].rearrange("p t j -> p j t"))
+            bounds(t)
+        for t in (0, 1):
+            codes(t)
+            cap(t, everything)
+        floor_pair(0, everything)
+        codes(2)
+        cap(2, everything)
+        codes(3)
         for h in halves:
+            cap(3, h)
+
+        def quantize(cols):
             nc.vector.quantize_mx(
-                x_codes[:, h].bitcast(FP8X4), x_scales[:, h], x_grouped[:, h, :].rearrange("p j t -> p (j t)")
+                x_codes[:, cols].bitcast(FP8X4), x_scales[:, cols], x_grouped[:, cols, :].rearrange("p j t -> p (j t)")
             )
 
-        hidden = [None] * PACK
-        for t in (0, 2, 3, 1):
-            bank = psum.tile([P, J], F32, name="bank%d" % t)
-            cols = slice(P * t, P * (t + 1))
+        floor_pair(2, halves[0])
+        floor_pair(2, slice(J // 2, 3 * J // 4))
+        quantize(halves[0])
+        floor_pair(2, slice(3 * J // 4, J))
+        quantize(halves[1])
+
+        def hidden(t, cols, name):
+            width = cols.stop - cols.start
+            bank = psum.tile([P, width], F32, name="bank_" + name, tag="bank_" + name)
+            rows = slice(P * t, P * (t + 1))
             nc.tensor.matmul_mx(
-                bank[:], lhsT=w_codes[:, cols].bitcast(FP8X4), lhsT_scale=w_scales[:, cols],
-                rhs=x_codes[:].bitcast(FP8X4), rhs_scale=x_scales[:], start=True, stop=True,
+                bank[:], lhsT=w_codes[:, rows].bitcast(FP8X4), lhsT_scale=w_scales[:, rows],
+                rhs=x_codes[:, cols].bitcast(FP8X4), rhs_scale=x_scales[:, cols], start=True, stop=True,
             )
-            a_t = pool.tile([P, J], F32, name="a%d" % t)
-            if t == 0:
-                nc.vector.tensor_copy(a_t[:], bank[:])
-            else:
-                nc.scalar.copy(a_t[:], bank[:])
-            hidden[t] = a_t
-        for t in (0, 2, 3):
-            nc.vector.tensor_copy(board[t][:].indirect(l5[:]), hidden[t][:])
-        nc.scalar.activation(board[1][:].indirect(l5[:]), hidden[1][:], COPY)
+            values = pool.tile([P, width], F32, name="a_" + name, tag="a_" + name)
+            nc.scalar.copy(values[:], bank[:])
+            return values
 
-        first = pool.tile([P, PACK, O], F32, name="first")
-        second = pool.tile([P, PACK, O], F32, name="second")
-        h_planes = pool.tile([P, PACK - 1, O], BF16, name="h_planes")
+        def entries(cols):
+            return l5[:, cols.start // 16 : cols.stop // 16]
+
+        for u, h in enumerate(halves):
+            for t in (0, 2):
+                nc.vector.tensor_copy(board[t][:].indirect(entries(h)), hidden(t, h, "%d%d" % (t, u))[:])
+            nc.scalar.activation(board[1][:].indirect(entries(h)), hidden(1, h, "1%d" % u)[:], COPY)
+        nc.vector.tensor_copy(board[3][:].indirect(l5[:]), hidden(3, everything, "3")[:])
+
+        picked = pool.tile([P, 2, PACK, O], F32, name="picked", tag="a_11")
+        first = picked[:, 0, :, :]
+        second = picked[:, 1, :, :]
         h_grouped = pool.tile([P, O, PACK], BF16, name="h_grouped", align_bytes=64)
         h_codes = pool.tile([P, O], U32, name="h_codes", align_bytes=64)
         h_scales = pool.tile([P, O], U8, name="h_scales", align_bytes=64)
         for t in range(PACK):
             nc.scalar.activation(first[:, t, :], board[t][:].indirect(l6[:]), COPY, scale=sa_t[:, t : t + 1])
             nc.scalar.activation(second[:, t, :], board[t][:].indirect(l7[:]), COPY, scale=sb_t[:, t : t + 1])
-        nc.vector.tensor_tensor(h_planes[:], first[:, 0:3, :], second[:, 0:3, :], MAX)
-        nc.vector.tensor_copy(h_grouped[:, :, 0:3], h_planes[:].rearrange("p t o -> p o t"))
-        nc.vector.tensor_tensor(h_grouped[:, :, 3], first[:, 3, :], second[:, 3, :], MAX)
+        for t in (0, 2):
+            nc.vector.tensor_tensor(
+                h_grouped[:, :, t : t + 2],
+                first[:, t : t + 2, :].rearrange("p t o -> p o t"),
+                second[:, t : t + 2, :].rearrange("p t o -> p o t"),
+                MAX,
+            )
         nc.vector.quantize_mx(h_codes[:].bitcast(FP8X4), h_scales[:], h_grouped[:].rearrange("p o t -> p (o t)"))
 
         for b in range(N // P):
-            bank = psum.tile([P, O], F32, name="ybank%d" % b)
+            bank = psum.tile([P, O], F32, name="ybank%d" % b, tag="bank_%d0" % (2 * b))
             nc.tensor.matmul_mx(
                 bank[:], lhsT=wb_codes[:, 2 * P * b : 2 * P * (b + 1)].bitcast(FP4X4),
                 lhsT_scale=wb_plane[:, P * b : P * (b + 1)],

@@ -55,14 +55,14 @@ def tile_picked_boundedcode_store_one_boardmixed_one_plain_kernel(
         tb_t[1] = table_tile(tb, 1, "tb1")
         wt_all = pool.tile([P, F], U32, name="wt_all")
         nc.sync.dma_start(wt_all[:].bitcast(I32), wt_words[0].rearrange("p n t -> p (n t)").bitcast(I32))
-        tb_t[2] = table_tile(tb, 2, "tb2")
+        l4 = list_tile(offs4, "l4")
         wt_rows = pool.tile([P, 2, F // 4], I32, name="wt_rows")
         for u in range(2):
             nc.sync.dma_start(
                 wt_rows[64 * u : 64 * u + PACK, :, :],
                 wt_scales[0].bitcast(I32)[8 * u : 8 * (u + 1), :].rearrange("(q i) c -> i q c", i=PACK),
             )
-        l4 = list_tile(offs4, "l4")
+        tb_t[2] = table_tile(tb, 2, "tb2")
         tb_t[3] = table_tile(tb, 3, "tb3")
         ga_t = column_tile(ga, "ga_t", nc.sync)
         l1 = list_tile(offs, "l1")
@@ -99,8 +99,18 @@ def tile_picked_boundedcode_store_one_boardmixed_one_plain_kernel(
         w_scales = pool.tile([P, R], U8, name="w_scales", align_bytes=64)
         halves = [slice(0, J // 2), slice(J // 2, J)]
 
-        nc.vector.tensor_copy(w_codes[:].rearrange("p (t m) -> p m t", t=PACK), wt_all[:].indirect(l4[:]))
-        nc.vector.tensor_copy(w_scales[:].rearrange("p (t m) -> p m t", t=PACK), wt_plane[:].indirect(l4[:]))
+        listed_codes = pool.tile([P, R], U32, name="listed_codes")
+        listed_scales = pool.tile([P, R], U8, name="listed_scales")
+        nc.vector.tensor_copy(listed_codes[:], wt_all[:].indirect(l4[:]))
+        nc.vector.tensor_copy(listed_scales[:], wt_plane[:].indirect(l4[:]))
+        nc.vector.tensor_copy(
+            w_codes[:].bitcast(I32).rearrange("p (t c i) -> p c t i", t=PACK, i=4),
+            listed_codes[:].bitcast(I32).rearrange("p (c i t) -> p c t i", t=PACK, i=4),
+        )
+        nc.vector.tensor_copy(
+            w_scales[:].rearrange("p (t c i) -> p c t i", t=PACK, i=16),
+            listed_scales[:].rearrange("p (c i t) -> p c t i", t=PACK, i=16),
+        )
 
         upper = pool.tile([P, PACK, J], F32, name="upper")
         lower = pool.tile([P, PACK, J], F32, name="lower")
@@ -119,9 +129,9 @@ def tile_picked_boundedcode_store_one_boardmixed_one_plain_kernel(
 
         def floor_pair(t, cols):
             nc.vector.tensor_tensor(
-                x_grouped[:, cols, t : t + 2],
-                capped[:, t : t + 2, cols].rearrange("p t j -> p j t"),
-                lower[:, t : t + 2, cols].rearrange("p t j -> p j t"),
+                x_grouped[:, cols, t : t + 2].rearrange("p (c i) t -> p c t i", i=2),
+                capped[:, t : t + 2, cols].rearrange("p t (c i) -> p c t i", i=2),
+                lower[:, t : t + 2, cols].rearrange("p t (c i) -> p c t i", i=2),
                 MAX,
             )
 
@@ -181,9 +191,9 @@ def tile_picked_boundedcode_store_one_boardmixed_one_plain_kernel(
             nc.scalar.activation(second[:, t, :], board[t][:].indirect(l7[:]), COPY, scale=sb_t[:, t : t + 1])
         for t in (0, 2):
             nc.vector.tensor_tensor(
-                h_grouped[:, :, t : t + 2],
-                first[:, t : t + 2, :].rearrange("p t o -> p o t"),
-                second[:, t : t + 2, :].rearrange("p t o -> p o t"),
+                h_grouped[:, :, t : t + 2].rearrange("p (c i) t -> p c t i", i=2),
+                first[:, t : t + 2, :].rearrange("p t (c i) -> p c t i", i=2),
+                second[:, t : t + 2, :].rearrange("p t (c i) -> p c t i", i=2),
                 MAX,
             )
         nc.vector.quantize_mx(h_codes[:].bitcast(FP8X4), h_scales[:], h_grouped[:].rearrange("p o t -> p (o t)"))

from contextlib import ExitStack

import concourse.mybir as mybir

F32 = mybir.dt.float32
BF16 = mybir.dt.bfloat16
I32 = mybir.dt.int32
U32 = mybir.dt.uint32
U16 = mybir.dt.uint16
U8 = mybir.dt.uint8
FP8X4 = mybir.dt.float8_e4m3fn_x4
FP4X4 = mybir.dt.float4_e2m1fn_x4
COPY = mybir.ActivationFunctionType.Copy
MIN = mybir.AluOpType.min
MAX = mybir.AluOpType.max

K, J, R, T, U, F, C, O, N = 512, 256, 512, 1024, 1024, 1024, 512, 128, 256
P = 128
PACK = 4
FLOPS = 2 * K * R * J + 2 * R * N * O


def tile_picked_boundedcode_store_one_boardmixed_one_plain_kernel(
    tc, ta, tb, ga, gb, gd, wt_words, wt_scales, sa, sb, wb_words, wb_scales,
    offs, offs2, offs3, offs4, offs5, offs6, offs7, out,
):
    nc = tc.nc
    with ExitStack() as ctx:
        lists = ctx.enter_context(tc.tile_pool(name="lists", bufs=1))
        pool = ctx.enter_context(tc.tile_pool(name="work", bufs=1))
        psum = ctx.enter_context(tc.psum_pool(name="psum", bufs=1))

        def list_tile(src, name):
            tile = lists.tile([P, src.shape[1]], U16, name=name)
            nc.sync.dma_start(tile[:], src)
            return tile

        def column_tile(src, name, queue):
            tile = pool.tile([P, PACK], F32, name=name)
            queue.dma_start(tile[:], src.rearrange("(p t) o -> p (t o)", t=PACK))
            return tile

        def table_tile(src, t, name):
            tile = pool.tile([P, src.shape[1]], F32, name=name)
            nc.sync.dma_start(tile[:], src.rearrange("(p t) c -> p t c", t=PACK)[:, t, :])
            return tile

        ta_t = [None] * PACK
        tb_t = [None] * PACK
        gb_t = column_tile(gb, "gb_t", nc.scalar)
        gd_t = column_tile(gd, "gd_t", nc.scalar)
        tb_t[0] = table_tile(tb, 0, "tb0")
        l2 = list_tile(offs2, "l2")
        l3 = list_tile(offs3, "l3")
        tb_t[1] = table_tile(tb, 1, "tb1")
        wt_all = pool.tile([P, F], U32, name="wt_all")
        nc.sync.dma_start(wt_all[:].bitcast(I32), wt_words[0].rearrange("p n t -> p (n t)").bitcast(I32))
        l4 = list_tile(offs4, "l4")
        wt_rows = pool.tile([P, 2, F // 4], I32, name="wt_rows")
        for u in range(2):
            nc.sync.dma_start(
                wt_rows[64 * u : 64 * u + PACK, :, :],
                wt_scales[0].bitcast(I32)[8 * u : 8 * (u + 1), :].rearrange("(q i) c -> i q c", i=PACK),
            )
        tb_t[2] = table_tile(tb, 2, "tb2")
        tb_t[3] = table_tile(tb, 3, "tb3")
        ga_t = column_tile(ga, "ga_t", nc.sync)
        l1 = list_tile(offs, "l1")
        for t in range(PACK):
            ta_t[t] = table_tile(ta, t, "ta%d" % t)
        l5 = list_tile(offs5, "l5")
        l6 = list_tile(offs6, "l6")
        l7 = list_tile(offs7, "l7")
        sa_t = column_tile(sa, "sa_t", nc.sync)
        sb_t = column_tile(sb, "sb_t", nc.sync)
        wb_codes = pool.tile([P, 2 * N], U8, name="wb_codes", align_bytes=64)
        nc.sync.dma_start(wb_codes[:].bitcast(I32), wb_words[0].bitcast(I32))
        wb_plane = pool.tile([P, N], U8, name="wb_plane", align_bytes=64)
        nc.vector.memset(wb_plane[:].bitcast(I32), 0)
        for q in range(4):
            nc.sync.dma_start(
                wb_plane[32 * q : 32 * q + PACK, :].bitcast(I32), wb_scales[0].bitcast(I32)[PACK * q : PACK * (q + 1), :]
            )

        board = [pool.tile([P, C], F32, name="board%d" % t) for t in range(PACK)]
        for t in range(PACK):
            nc.vector.memset(board[t][:], 0.0)
        wt_plane = pool.tile([P, F], U8, name="wt_plane")
        nc.vector.memset(wt_plane[:].bitcast(I32), 0)
        for q in range(4):
            nc.vector.tensor_copy(
                wt_plane[32 * q : 32 * q + PACK, :].bitcast(I32), wt_rows[64 * (q // 2) : 64 * (q // 2) + PACK, q % 2, :]
            )

        x_grouped = pool.tile([P, J, PACK], BF16, name="x_grouped", align_bytes=64)
        x_codes = pool.tile([P, J], U32, name="x_codes", align_bytes=64)
        x_scales = pool.tile([P, J], U8, name="x_scales", align_bytes=64)
        w_codes = pool.tile([P, R], U32, name="w_codes", align_bytes=64)
        w_scales = pool.tile([P, R], U8, name="w_scales", align_bytes=64)
        halves = [slice(0, J // 2), slice(J // 2, J)]

        listed_codes = pool.tile([P, R], U32, name="listed_codes")
        listed_scales = pool.tile([P, R], U8, name="listed_scales")
        nc.vector.tensor_copy(listed_codes[:], wt_all[:].indirect(l4[:]))
        nc.vector.tensor_copy(listed_scales[:], wt_plane[:].indirect(l4[:]))
        nc.vector.tensor_copy(
            w_codes[:].bitcast(I32).rearrange("p (t c i) -> p c t i", t=PACK, i=4),
            listed_codes[:].bitcast(I32).rearrange("p (c i t) -> p c t i", t=PACK, i=4),
        )
        nc.vector.tensor_copy(
            w_scales[:].rearrange("p (t c i) -> p c t i", t=PACK, i=16),
            listed_scales[:].rearrange("p (c i t) -> p c t i", t=PACK, i=16),
        )

        upper = pool.tile([P, PACK, J], F32, name="upper")
        lower = pool.tile([P, PACK, J], F32, name="lower")
        coded = pool.tile([P, PACK, J], F32, name="coded")
        capped = pool.tile([P, PACK, J], F32, name="capped")

        def bounds(t):
            nc.scalar.activation(upper[:, t, :], tb_t[t][:].indirect(l2[:]), COPY, scale=gb_t[:, t : t + 1])
            nc.scalar.activation(lower[:, t, :], tb_t[t][:].indirect(l3[:]), COPY, scale=gd_t[:, t : t + 1])

        def codes(t):
            nc.scalar.activation(coded[:, t, :], ta_t[t][:].indirect(l1[:]), COPY, scale=ga_t[:, t : t + 1])

        def cap(t, cols):
            nc.vector.tensor_tensor(capped[:, t, cols], coded[:, t, cols], upper[:, t, cols], MIN)

        def floor_pair(t, cols):
            nc.vector.tensor_tensor(
                x_grouped[:, cols, t : t + 2].rearrange("p (c i) t -> p c t i", i=2),
                capped[:, t : t + 2, cols].rearrange("p t (c i) -> p c t i", i=2),
                lower[:, t : t + 2, cols].rearrange("p t (c i) -> p c t i", i=2),
                MAX,
            )

        everything = slice(0, J)
        for t in range(PACK):
            bounds(t)
        for t in (0, 1):
            codes(t)
            cap(t, everything)
        floor_pair(0, everything)
        codes(2)
        cap(2, everything)
        codes(3)
        for h in halves:
            cap(3, h)

        def quantize(cols):
            nc.vector.quantize_mx(
                x_codes[:, cols].bitcast(FP8X4), x_scales[:, cols], x_grouped[:, cols, :].rearrange("p j t -> p (j t)")
            )

        floor_pair(2, halves[0])
        floor_pair(2, slice(J // 2, 3 * J // 4))
        quantize(halves[0])
        floor_pair(2, slice(3 * J // 4, J))
        quantize(halves[1])

        def hidden(t, cols, name):
            width = cols.stop - cols.start
            bank = psum.tile([P, width], F32, name="bank_" + name, tag="bank_" + name)
            rows = slice(P * t, P * (t + 1))
            nc.tensor.matmul_mx(
                bank[:], lhsT=w_codes[:, rows].bitcast(FP8X4), lhsT_scale=w_scales[:, rows],
                rhs=x_codes[:, cols].bitcast(FP8X4), rhs_scale=x_scales[:, cols], start=True, stop=True,
            )
            values = pool.tile([P, width], F32, name="a_" + name, tag="a_" + name)
            nc.scalar.copy(values[:], bank[:])
            return values

        def entries(cols):
            return l5[:, cols.start // 16 : cols.stop // 16]

        for u, h in enumerate(halves):
            for t in (0, 2):
                nc.vector.tensor_copy(board[t][:].indirect(entries(h)), hidden(t, h, "%d%d" % (t, u))[:])
            nc.scalar.activation(board[1][:].indirect(entries(h)), hidden(1, h, "1%d" % u)[:], COPY)
        nc.vector.tensor_copy(board[3][:].indirect(l5[:]), hidden(3, everything, "3")[:])

        picked = pool.tile([P, 2, PACK, O], F32, name="picked", tag="a_11")
        first = picked[:, 0, :, :]
        second = picked[:, 1, :, :]
        h_grouped = pool.tile([P, O, PACK], BF16, name="h_grouped", align_bytes=64)
        h_codes = pool.tile([P, O], U32, name="h_codes", align_bytes=64)
        h_scales = pool.tile([P, O], U8, name="h_scales", align_bytes=64)
        for t in range(PACK):
            nc.scalar.activation(first[:, t, :], board[t][:].indirect(l6[:]), COPY, scale=sa_t[:, t : t + 1])
            nc.scalar.activation(second[:, t, :], board[t][:].indirect(l7[:]), COPY, scale=sb_t[:, t : t + 1])
        for t in (0, 2):
            nc.vector.tensor_tensor(
                h_grouped[:, :, t : t + 2].rearrange("p (c i) t -> p c t i", i=2),
                first[:, t : t + 2, :].rearrange("p t (c i) -> p c t i", i=2),
                second[:, t : t + 2, :].rearrange("p t (c i) -> p c t i", i=2),
                MAX,
            )
        nc.vector.quantize_mx(h_codes[:].bitcast(FP8X4), h_scales[:], h_grouped[:].rearrange("p o t -> p (o t)"))

        for b in range(N // P):
            bank = psum.tile([P, O], F32, name="ybank%d" % b, tag="bank_%d0" % (2 * b))
            nc.tensor.matmul_mx(
                bank[:], lhsT=wb_codes[:, 2 * P * b : 2 * P * (b + 1)].bitcast(FP4X4),
                lhsT_scale=wb_plane[:, P * b : P * (b + 1)],
                rhs=h_codes[:].bitcast(FP8X4), rhs_scale=h_scales[:], start=True, stop=True,
            )
            y = pool.tile([P, O], F32, name="y%d" % b)
            if b == 0:
                nc.scalar.copy(y[:], bank[:])
                nc.scalar.dma_start(out[P * b : P * (b + 1), :], y[:])
            else:
                nc.vector.tensor_copy(y[:], bank[:])
                nc.sync.dma_start(out[P * b : P * (b + 1), :], y[:])
